import numpy as np
import ml_dtypes


def mxq(x, axis, fmt="e4m3"):
    dtype, down = {"e4m3": (ml_dtypes.float8_e4m3fn, 7), "e5m2": (ml_dtypes.float8_e5m2, 14)}[fmt]
    v = np.moveaxis(np.asarray(x, np.float32).astype(ml_dtypes.bfloat16).astype(np.float64), axis, -1)
    blocks = v.reshape(v.shape[:-1] + (-1, 32))
    amax = np.abs(blocks).max(-1, keepdims=True)
    byte = np.maximum(np.where(amax > 0, np.frexp(amax)[1] - 1 + 127, 0) - down, 1)
    scale = np.exp2(byte - 127.0)
    codes = (blocks / scale).astype(np.float32).astype(dtype).astype(np.float64)
    return np.moveaxis((codes * scale).reshape(v.shape), -1, axis)


WIDE = False


def mx_kscale(k):
    if not WIDE:
        return np.ones(k)
    levels = np.array([10, -10, 5, -5, 0])
    if k % 512:
        return np.exp2(np.random.permutation(np.resize(levels, k // 32))).repeat(32)
    a = np.empty((k // 512, 16))
    for p in range(k // 512):
        a[p, :8] = np.random.permutation(np.resize(levels, 8))
        for g in range(8):
            far = levels[np.abs(levels - a[p, g]) >= 10]
            a[p, g + 8] = far[np.random.randint(len(far))]
    return np.exp2(a.ravel()).repeat(32)


def f64(x):
    return np.asarray(x).astype(np.float64)


def striped(idx):
    return np.tile(idx.reshape(-1, 16).T, (8, 1)).astype(np.uint16)


def unstriped(offs):
    return offs[:16].T.reshape(-1).astype(np.int64)


def striped8(idx):
    return np.concatenate([x.reshape(-1, 16).T for x in idx]).astype(np.uint16)


def runs(offs, k):
    lists = np.stack([offs[16 * r : 16 * r + 16].T.reshape(-1) for r in range(8)]).astype(np.int64)
    return lists[np.arange(k) % 512 // 64]


def pack_weight(w):
    k, n = w.shape
    w = f64(np.asarray(w, np.float32).astype(ml_dtypes.bfloat16)).reshape(k // 32, 32, n)
    amax = np.abs(w).max(1)
    byte = np.clip(np.where(amax > 0, np.frexp(amax)[1] - 1 + 127 - 7, 1), 1, 254)
    scaled = (w * np.exp2(127.0 - byte)[:, None, :]).reshape(k, n).astype(np.float32)
    words = np.ascontiguousarray(scaled.reshape(k // 512, 128, 4, n).transpose(0, 1, 3, 2)).astype(ml_dtypes.float8_e4m3fn).view(np.uint8)
    return words, np.ascontiguousarray(byte.astype(np.uint8).reshape(k // 512, 16, n))


def unpack_weight(words, scales):
    g, p, n, _ = words.shape
    vals = np.ascontiguousarray(words).view(ml_dtypes.float8_e4m3fn).astype(np.float64) * np.repeat(np.exp2(scales.astype(np.float64) - 127.0), 8, axis=1)[..., None]
    return vals.transpose(0, 1, 3, 2).reshape(g * 512, n)


K, T, S, V, H, C = 512, 2048, 512, 256, 512, 512


def setup_inputs():
    n = np.random.standard_normal
    s = mx_kscale(K)[:, None]
    packed_xT = pack_weight(n((K, T)) * s)
    return {
        "x_words": packed_xT[0],
        "x_scales": packed_xT[1],
        "w1": (n((K, H)) / np.sqrt(K) / s).astype(np.float32),
        "gs": (np.random.uniform(0.5, 1.5, (K, 1)) / s).astype(np.float32),
        "offs": striped(np.random.permutation(T)[:S]),
        "i_l": striped8(np.stack([np.random.permutation(S)[:V] for _ in range(8)])),
        "k_l": striped8(np.stack([np.random.permutation(S)[:V] for _ in range(8)])),
        "j_l": striped8(np.stack([np.random.permutation(S)[:V] for _ in range(8)])),
        "cand": striped(np.random.permutation(T)[:C]),
    }


def reference(x_words, x_scales, w1, gs, offs, i_l, k_l, j_l, cand):
    x_cand = unpack_weight(x_words, x_scales)[:, unstriped(cand)]
    xq = unpack_weight(x_words, x_scales)[:, unstriped(offs)]
    y = mxq(f64(w1), 0, "e4m3").T @ xq
    a = y[np.arange(H)[:, None], runs(i_l, H)] - (y[np.arange(H)[:, None], runs(k_l, H)])
    b = y[np.arange(H)[:, None], runs(j_l, H)] - (y[np.arange(H)[:, None], runs(k_l, H)])
    z = f64(gs) * ((a * b) / (np.sqrt(((a) ** 2 + 0.25) * ((b) ** 2 + 0.25))))
    return 0.0625 * ((x_cand.T @ mxq(z, 0, "e4m3")))

@@ -1,0 +1,205 @@
+from contextlib import ExitStack
+
+import concourse.mybir as mybir
+
+K, T, S, V, H, C = 512, 2048, 512, 256, 512, 512
+FLOPS = 2 * K * H * S + 2 * K * C * V
+
+F32 = mybir.dt.float32
+BF16 = mybir.dt.bfloat16
+I32 = mybir.dt.int32
+U32 = mybir.dt.uint32
+U16 = mybir.dt.uint16
+U8 = mybir.dt.uint8
+FP8X4 = mybir.dt.float8_e4m3fn_x4
+ALU = mybir.AluOpType
+ACT = mybir.ActivationFunctionType
+
+P = 128
+PACK = 4
+HALF_M = 64
+HALF_V = V // 2
+M_ON_VECTOR = 40
+
+
+def tile_picked_bondang_none_p_kernel(tc, x_words, x_scales, w1, gs, offs, i_l, k_l, j_l, cand, out):
+    nc = tc.nc
+    with ExitStack() as ctx:
+        keep = ctx.enter_context(tc.tile_pool(name="keep", bufs=1))
+        psum = ctx.enter_context(tc.psum_pool(name="psum", bufs=1))
+
+        def load_list(name, src):
+            tile = keep.tile(list(src.shape), U16, name=name)
+            nc.sync.dma_start(tile[:], src)
+            return tile
+
+        table_scales = keep.tile([P, T], U8, name="table_scales", align_bytes=64)
+        nc.vector.memset(table_scales[:].bitcast(I32), 0)
+        quarter = keep.tile([P, 1], F32, name="quarter")
+        nc.gpsimd.memset(quarter[:], 0.25)
+
+        offs_sb = load_list("offs_sb", offs)
+        cand_sb = load_list("cand_sb", cand)
+        table_words = keep.tile([P, T], I32, name="table_words", align_bytes=64)
+        nc.sync.dma_start(table_words[:], x_words[0].rearrange("p n r -> p (n r)").bitcast(I32))
+        for q in range(4):
+            nc.scalar.dma_start(table_scales[32 * q : 32 * q + 4, :].bitcast(I32), x_scales[0, 4 * q : 4 * q + 4, :].bitcast(I32))
+        w_view = w1.rearrange("(p j) c -> p j c", j=PACK)
+        w_raw = []
+        for h in range(2):
+            raw = keep.tile([P, PACK, H // 2], F32, name=f"w_raw{h}")
+            nc.sync.dma_start(raw[:], w_view[:, :, h * (H // 2) : (h + 1) * (H // 2)])
+            w_raw.append(raw)
+        k_sb = load_list("k_sb", k_l)
+        i_sb = load_list("i_sb", i_l)
+        j_sb = load_list("j_sb", j_l)
+        gs_sb = keep.tile([P, PACK], F32, name="gs_sb")
+        nc.sync.dma_start(gs_sb[:], gs.rearrange("(p t) o -> p (t o)", t=PACK))
+
+        warm = keep.tile([P, 1], F32, name="warm")
+        nc.scalar.activation(warm[:], quarter[:], ACT.Abs_reciprocal_sqrt, bias=quarter[:])
+
+        def gather_packed(name, table, dtype, offsets):
+            picked = keep.tile([P, S], dtype, name=name, align_bytes=64)
+            nc.vector.tensor_copy(picked[:], table.indirect(offsets[:]))
+            return picked
+
+        xq_scales = gather_packed("xq_scales", table_scales[:], U8, offs_sb)
+        xc_scales = gather_packed("xc_scales", table_scales[:], U8, cand_sb)
+        xq_words = gather_packed("xq_words", table_words[:].bitcast(U32), U32, offs_sb)
+        xc_words = gather_packed("xc_words", table_words[:].bitcast(U32), U32, cand_sb)
+
+        w_codes = keep.tile([P, H], U32, name="w_codes", align_bytes=64)
+        w_scales = keep.tile([P, H], U8, name="w_scales", align_bytes=64)
+        for h in range(2):
+            grouped = keep.tile([P, PACK, HALF_M, PACK], BF16, name=f"w_grouped{h}", align_bytes=64)
+            dst = grouped[:].rearrange("p t m j -> p m t j")
+            src = w_raw[h][:].rearrange("p j (m t) -> p m t j", t=PACK)
+            if h == 0:
+                nc.scalar.copy(dst, src)
+            else:
+                nc.vector.tensor_copy(dst[:, :M_ON_VECTOR], src[:, :M_ON_VECTOR])
+                nc.scalar.copy(dst[:, M_ON_VECTOR:], src[:, M_ON_VECTOR:])
+            for t in range(PACK):
+                cols = slice(t * P + h * HALF_M, t * P + (h + 1) * HALF_M)
+                nc.vector.quantize_mx(
+                    out=w_codes[:, cols].bitcast(FP8X4),
+                    scales=w_scales[:, cols],
+                    in_=grouped[:, t].rearrange("p m j -> p (m j)"),
+                )
+
+        def project(t, cols, name):
+            acc = psum.tile([P, cols.stop - cols.start], F32, name=name)
+            rows = slice(t * P, (t + 1) * P)
+            nc.tensor.matmul_mx(
+                out=acc[:],
+                lhsT=w_codes[:, rows].bitcast(FP8X4),
+                lhsT_scale=w_scales[:, rows],
+                rhs=xq_words[:, cols].bitcast(FP8X4),
+                rhs_scale=xq_scales[:, cols],
+                start=True,
+                stop=True,
+            )
+            return acc
+
+        y = [keep.tile([P, S], F32, name=f"y{t}") for t in range(PACK)]
+        lo, hi = slice(0, S // 2), slice(S // 2, S)
+        nc.scalar.copy(y[0][:, lo], project(0, lo, "y0_lo")[:])
+        nc.vector.tensor_copy(y[0][:, hi], project(0, hi, "y0_hi")[:])
+        for t in range(1, PACK):
+            nc.scalar.copy(y[t][:], project(t, slice(0, S), f"y{t}_acc")[:])
+
+        tip = [keep.tile([P, V], F32, name=f"tip{t}") for t in range(PACK)]
+        prod = keep.tile([P, PACK, V], F32, name="prod")
+        inv = keep.tile([P, PACK, V], F32, name="inv")
+
+        def gather_tip(t):
+            nc.vector.tensor_copy(tip[t][:], y[t][:].indirect(k_sb[:]))
+
+        def bonds(t, v0, n):
+            ab = keep.tile([P, 2, n], F32, name=f"ab{t}_{v0}")
+            for s, lst in enumerate((i_sb, j_sb)):
+                nc.vector.tensor_tensor(ab[:, s, :], y[t][:].indirect(lst[:, v0 // 16 : (v0 + n) // 16]), tip[t][:, v0 : v0 + n], ALU.subtract)
+            sq = keep.tile([P, 2, n], F32, name=f"sq{t}_{v0}")
+            nc.scalar.activation(sq[:], ab[:], ACT.Square)
+            roots = keep.tile([P, 2, n], F32, name=f"roots{t}_{v0}")
+            nc.scalar.activation(roots[:], sq[:], ACT.Abs_reciprocal_sqrt, bias=quarter[:])
+            return (t, v0, n, ab, roots)
+
+        def numerator(piece):
+            t, v0, n, ab, roots = piece
+            nc.vector.scalar_tensor_tensor(prod[:, t, v0 : v0 + n], ab[:, 0, :], gs_sb[:, t : t + 1], ab[:, 1, :], ALU.mult, ALU.mult)
+
+        def denominator(piece):
+            t, v0, n, ab, roots = piece
+            nc.vector.tensor_tensor(inv[:, t, v0 : v0 + n], roots[:, 0, :], roots[:, 1, :], ALU.mult)
+
+        def weigh(h):
+            vs = slice(h * HALF_V, (h + 1) * HALF_V)
+            z = keep.tile([P, HALF_V, PACK], BF16, name=f"z{h}", align_bytes=64)
+            nc.vector.tensor_tensor(
+                z[:].rearrange("p (c i) t -> p c t i", i=4),
+                prod[:, :, vs].rearrange("p t (c i) -> p c t i", i=4),
+                inv[:, :, vs].rearrange("p t (c i) -> p c t i", i=4),
+                ALU.mult,
+            )
+            return z
+
+        def quantize_z(h, z):
+            codes = keep.tile([P, HALF_V], U32, name=f"z_codes{h}", align_bytes=64)
+            scales = keep.tile([P, HALF_V], U8, name=f"z_scales{h}", align_bytes=64)
+            nc.vector.quantize_mx(out=codes[:].bitcast(FP8X4), scales=scales[:], in_=z[:].rearrange("p v t -> p (v t)"))
+            return codes, scales
+
+        out_view = out.rearrange("(b p) v -> p b v", p=P)
+
+        def score(h, codes, scales, blocks, name):
+            acc = psum.tile([P, len(blocks), HALF_V], F32, name=name)
+            for n, b in enumerate(blocks):
+                rows = slice(b * P, (b + 1) * P)
+                nc.tensor.matmul_mx(
+                    out=acc[:, n, :],
+                    lhsT=xc_words[:, rows].bitcast(FP8X4),
+                    lhsT_scale=xc_scales[:, rows],
+                    rhs=codes[:].bitcast(FP8X4),
+                    rhs_scale=scales[:],
+                    start=True,
+                    stop=True,
+                )
+            return acc
+
+        def store(h, acc, blocks, on_vector):
+            res = keep.tile([P, len(blocks), HALF_V], F32, name=f"res{h}_{blocks[0]}")
+            if on_vector:
+                nc.vector.tensor_scalar(res[:], acc[:], 0.0625, None, ALU.mult)
+            else:
+                nc.scalar.activation(res[:], acc[:], ACT.Copy, scale=0.0625)
+            queue = nc.sync if on_vector or h == 0 else nc.scalar
+            queue.dma_start(out_view[:, blocks[0] : blocks[-1] + 1, h * HALF_V : (h + 1) * HALF_V], res[:])
+
+        gather_tip(0)
+        gather_tip(1)
+        p0 = bonds(0, 0, V)
+        gather_tip(2)
+        p1 = bonds(1, 0, V)
+        numerator(p0)
+        gather_tip(3)
+        denominator(p0)
+        p2 = bonds(2, 0, V)
+        numerator(p1)
+        denominator(p1)
+        p3a = bonds(3, 0, HALF_V)
+        numerator(p2)
+        p3b = bonds(3, HALF_V, HALF_V)
+        numerator(p3a)
+        denominator(p2)
+        denominator(p3a)
+        numerator(p3b)
+        z0 = weigh(0)
+        denominator(p3b)
+        q0 = quantize_z(0, z0)
+        z1 = weigh(1)
+        store(0, score(0, q0[0], q0[1], [0, 1, 2, 3], "out0"), [0, 1, 2, 3], False)
+        q1 = quantize_z(1, z1)
+        store(1, score(1, q1[0], q1[1], [0, 1], "out1a"), [0, 1], False)
+        store(1, score(1, q1[0], q1[1], [2, 3], "out1b"), [2, 3], True)

@@ -19,7 +19,6 @@ P = 128
 PACK = 4
 HALF_M = 64
 HALF_V = V // 2
-M_ON_VECTOR = 40
 
 
 def tile_picked_bondang_none_p_kernel(tc, x_words, x_scales, w1, gs, offs, i_l, k_l, j_l, cand, out):
@@ -38,18 +37,16 @@ def tile_picked_bondang_none_p_kernel(tc, x_words, x_scales, w1, gs, offs, i_l, 
         quarter = keep.tile([P, 1], F32, name="quarter")
         nc.gpsimd.memset(quarter[:], 0.25)
 
+        w_view = w1.rearrange("(p j) c -> p j c", j=PACK)
+        w_raw = [keep.tile([P, PACK, H // 2], F32, name=f"w_raw{h}") for h in range(2)]
         offs_sb = load_list("offs_sb", offs)
+        nc.sync.dma_start(w_raw[0][:], w_view[:, :, : H // 2])
+        for q in range(4):
+            nc.sync.dma_start(table_scales[32 * q : 32 * q + 4, :].bitcast(I32), x_scales[0, 4 * q : 4 * q + 4, :].bitcast(I32))
         cand_sb = load_list("cand_sb", cand)
+        nc.sync.dma_start(w_raw[1][:], w_view[:, :, H // 2 :])
         table_words = keep.tile([P, T], I32, name="table_words", align_bytes=64)
         nc.sync.dma_start(table_words[:], x_words[0].rearrange("p n r -> p (n r)").bitcast(I32))
-        for q in range(4):
-            nc.scalar.dma_start(table_scales[32 * q : 32 * q + 4, :].bitcast(I32), x_scales[0, 4 * q : 4 * q + 4, :].bitcast(I32))
-        w_view = w1.rearrange("(p j) c -> p j c", j=PACK)
-        w_raw = []
-        for h in range(2):
-            raw = keep.tile([P, PACK, H // 2], F32, name=f"w_raw{h}")
-            nc.sync.dma_start(raw[:], w_view[:, :, h * (H // 2) : (h + 1) * (H // 2)])
-            w_raw.append(raw)
         k_sb = load_list("k_sb", k_l)
         i_sb = load_list("i_sb", i_l)
         j_sb = load_list("j_sb", j_l)
@@ -66,27 +63,25 @@ def tile_picked_bondang_none_p_kernel(tc, x_words, x_scales, w1, gs, offs, i_l, 
 
         xq_scales = gather_packed("xq_scales", table_scales[:], U8, offs_sb)
         xc_scales = gather_packed("xc_scales", table_scales[:], U8, cand_sb)
-        xq_words = gather_packed("xq_words", table_words[:].bitcast(U32), U32, offs_sb)
-        xc_words = gather_packed("xc_words", table_words[:].bitcast(U32), U32, cand_sb)
 
         w_codes = keep.tile([P, H], U32, name="w_codes", align_bytes=64)
         w_scales = keep.tile([P, H], U8, name="w_scales", align_bytes=64)
+        grouped = keep.tile([P, PACK, P, PACK], BF16, name="w_grouped", align_bytes=64)
         for h in range(2):
-            grouped = keep.tile([P, PACK, HALF_M, PACK], BF16, name=f"w_grouped{h}", align_bytes=64)
-            dst = grouped[:].rearrange("p t m j -> p m t j")
-            src = w_raw[h][:].rearrange("p j (m t) -> p m t j", t=PACK)
-            if h == 0:
-                nc.scalar.copy(dst, src)
-            else:
-                nc.vector.tensor_copy(dst[:, :M_ON_VECTOR], src[:, :M_ON_VECTOR])
-                nc.scalar.copy(dst[:, M_ON_VECTOR:], src[:, M_ON_VECTOR:])
-            for t in range(PACK):
-                cols = slice(t * P + h * HALF_M, t * P + (h + 1) * HALF_M)
-                nc.vector.quantize_mx(
-                    out=w_codes[:, cols].bitcast(FP8X4),
-                    scales=w_scales[:, cols],
-                    in_=grouped[:, t].rearrange("p m j -> p (m j)"),
-                )
+            nc.scalar.copy(
+                grouped[:, :, h * HALF_M : (h + 1) * HALF_M, :].rearrange("p t m j -> p m t j"),
+                w_raw[h][:].rearrange("p j (m t) -> p m t j", t=PACK),
+            )
+        for t in range(PACK):
+            cols = slice(t * P, (t + 1) * P)
+            nc.vector.quantize_mx(
+                out=w_codes[:, cols].bitcast(FP8X4),
+                scales=w_scales[:, cols],
+                in_=grouped[:, t].rearrange("p m j -> p (m j)"),
+            )
+
+        xq_words = gather_packed("xq_words", table_words[:].bitcast(U32), U32, offs_sb)
+        xc_words = gather_packed("xc_words", table_words[:].bitcast(U32), U32, cand_sb)
 
         def project(t, cols, name):
             acc = psum.tile([P, cols.stop - cols.start], F32, name=name)
@@ -105,7 +100,7 @@ def tile_picked_bondang_none_p_kernel(tc, x_words, x_scales, w1, gs, offs, i_l, 
         y = [keep.tile([P, S], F32, name=f"y{t}") for t in range(PACK)]
         lo, hi = slice(0, S // 2), slice(S // 2, S)
         nc.scalar.copy(y[0][:, lo], project(0, lo, "y0_lo")[:])
-        nc.vector.tensor_copy(y[0][:, hi], project(0, hi, "y0_hi")[:])
+        nc.scalar.copy(y[0][:, hi], project(0, hi, "y0_hi")[:])
         for t in range(1, PACK):
             nc.scalar.copy(y[t][:], project(t, slice(0, S), f"y{t}_acc")[:])
 

@@ -72,15 +72,18 @@ def tile_picked_bondang_none_p_kernel(tc, x_words, x_scales, w1, gs, offs, i_l, 
                 grouped[:, :, h * HALF_M : (h + 1) * HALF_M, :].rearrange("p t m j -> p m t j"),
                 w_raw[h][:].rearrange("p j (m t) -> p m t j", t=PACK),
             )
-        for t in range(PACK):
-            cols = slice(t * P, (t + 1) * P)
-            nc.vector.quantize_mx(
-                out=w_codes[:, cols].bitcast(FP8X4),
-                scales=w_scales[:, cols],
-                in_=grouped[:, t].rearrange("p m j -> p (m j)"),
-            )
+        nc.vector.quantize_mx(
+            out=w_codes[:].bitcast(FP8X4),
+            scales=w_scales[:],
+            in_=grouped[:].rearrange("p t m j -> p (t m j)"),
+        )
 
-        xq_words = gather_packed("xq_words", table_words[:].bitcast(U32), U32, offs_sb)
+        xq_words = keep.tile([P, S], U32, name="xq_words", align_bytes=64)
+        for h in range(2):
+            nc.vector.tensor_copy(
+                xq_words[:, h * (S // 2) : (h + 1) * (S // 2)],
+                table_words[:].bitcast(U32).indirect(offs_sb[:, h * (S // 32) : (h + 1) * (S // 32)]),
+            )
         xc_words = gather_packed("xc_words", table_words[:].bitcast(U32), U32, cand_sb)
 
         def project(t, cols, name):
@@ -108,26 +111,28 @@ def tile_picked_bondang_none_p_kernel(tc, x_words, x_scales, w1, gs, offs, i_l, 
         prod = keep.tile([P, PACK, V], F32, name="prod")
         inv = keep.tile([P, PACK, V], F32, name="inv")
 
-        def gather_tip(t):
-            nc.vector.tensor_copy(tip[t][:], y[t][:].indirect(k_sb[:]))
+        def gather_tip(t, v0, n):
+            nc.vector.tensor_copy(tip[t][:, v0 : v0 + n], y[t][:].indirect(k_sb[:, v0 // 16 : (v0 + n) // 16]))
 
-        def bonds(t, v0, n):
-            ab = keep.tile([P, 2, n], F32, name=f"ab{t}_{v0}")
-            for s, lst in enumerate((i_sb, j_sb)):
-                nc.vector.tensor_tensor(ab[:, s, :], y[t][:].indirect(lst[:, v0 // 16 : (v0 + n) // 16]), tip[t][:, v0 : v0 + n], ALU.subtract)
-            sq = keep.tile([P, 2, n], F32, name=f"sq{t}_{v0}")
-            nc.scalar.activation(sq[:], ab[:], ACT.Square)
-            roots = keep.tile([P, 2, n], F32, name=f"roots{t}_{v0}")
-            nc.scalar.activation(roots[:], sq[:], ACT.Abs_reciprocal_sqrt, bias=quarter[:])
-            return (t, v0, n, ab, roots)
+        ab = [keep.tile([P, 2, V], F32, name=f"ab{t}") for t in range(PACK)]
+        squares = [keep.tile([P, 2, V], F32, name=f"squares{t}") for t in range(PACK)]
+        roots = keep.tile([P, PACK, 2, V], F32, name="roots")
 
-        def numerator(piece):
-            t, v0, n, ab, roots = piece
-            nc.vector.scalar_tensor_tensor(prod[:, t, v0 : v0 + n], ab[:, 0, :], gs_sb[:, t : t + 1], ab[:, 1, :], ALU.mult, ALU.mult)
+        def bond(t, s, v0, n):
+            lst = (i_sb, j_sb)[s]
+            nc.vector.tensor_tensor(ab[t][:, s, v0 : v0 + n], y[t][:].indirect(lst[:, v0 // 16 : (v0 + n) // 16]), tip[t][:, v0 : v0 + n], ALU.subtract)
 
-        def denominator(piece):
-            t, v0, n, ab, roots = piece
-            nc.vector.tensor_tensor(inv[:, t, v0 : v0 + n], roots[:, 0, :], roots[:, 1, :], ALU.mult)
+        def square(t, v0, n):
+            nc.scalar.activation(squares[t][:, :, v0 : v0 + n], ab[t][:, :, v0 : v0 + n], ACT.Square)
+
+        def root(t, v0, n):
+            nc.scalar.activation(roots[:, t, :, v0 : v0 + n], squares[t][:, :, v0 : v0 + n], ACT.Abs_reciprocal_sqrt, bias=quarter[:])
+
+        def numerator(t, v0, n):
+            nc.vector.scalar_tensor_tensor(prod[:, t, v0 : v0 + n], ab[t][:, 0, v0 : v0 + n], gs_sb[:, t : t + 1], ab[t][:, 1, v0 : v0 + n], ALU.mult, ALU.mult)
+
+        def denominator(t0, t1, v0, n):
+            nc.vector.tensor_tensor(inv[:, t0:t1, v0 : v0 + n], roots[:, t0:t1, 0, v0 : v0 + n], roots[:, t0:t1, 1, v0 : v0 + n], ALU.mult)
 
         def weigh(h):
             vs = slice(h * HALF_V, (h + 1) * HALF_V)
@@ -172,26 +177,42 @@ def tile_picked_bondang_none_p_kernel(tc, x_words, x_scales, w1, gs, offs, i_l, 
             queue = nc.sync if on_vector or h == 0 else nc.scalar
             queue.dma_start(out_view[:, blocks[0] : blocks[-1] + 1, h * HALF_V : (h + 1) * HALF_V], res[:])
 
-        gather_tip(0)
-        gather_tip(1)
-        p0 = bonds(0, 0, V)
-        gather_tip(2)
-        p1 = bonds(1, 0, V)
-        numerator(p0)
-        gather_tip(3)
-        denominator(p0)
-        p2 = bonds(2, 0, V)
-        numerator(p1)
-        denominator(p1)
-        p3a = bonds(3, 0, HALF_V)
-        numerator(p2)
-        p3b = bonds(3, HALF_V, HALF_V)
-        numerator(p3a)
-        denominator(p2)
-        denominator(p3a)
-        numerator(p3b)
+        gather_tip(0, 0, HALF_V)
+        gather_tip(0, HALF_V, HALF_V)
+        gather_tip(1, 0, V)
+        bond(0, 0, 0, HALF_V)
+        bond(0, 0, HALF_V, HALF_V)
+        bond(0, 1, 0, V)
+        square(0, 0, V)
+        root(0, 0, V)
+        gather_tip(2, 0, V)
+        numerator(0, 0, V)
+        bond(1, 0, 0, V)
+        bond(1, 1, 0, V)
+        square(1, 0, V)
+        root(1, 0, V)
+        gather_tip(3, 0, V)
+        numerator(1, 0, V)
+        bond(2, 0, 0, V)
+        bond(2, 1, 0, V)
+        square(2, 0, V)
+        bond(3, 0, 0, HALF_V)
+        bond(3, 1, 0, HALF_V)
+        square(3, 0, HALF_V)
+        root(3, 0, HALF_V)
+        root(2, 0, V)
+        bond(3, 0, HALF_V, HALF_V)
+        bond(3, 1, HALF_V, HALF_V)
+        square(3, HALF_V, HALF_V)
+        root(3, HALF_V, HALF_V)
+        numerator(3, 0, HALF_V)
+        numerator(2, 0, V)
+        numerator(3, HALF_V, HALF_V)
+        denominator(3, 4, 0, HALF_V)
+        denominator(0, 3, 0, HALF_V)
+        denominator(0, 3, HALF_V, HALF_V)
         z0 = weigh(0)
-        denominator(p3b)
+        denominator(3, 4, HALF_V, HALF_V)
         q0 = quantize_z(0, z0)
         z1 = weigh(1)
         store(0, score(0, q0[0], q0[1], [0, 1, 2, 3], "out0"), [0, 1, 2, 3], False)

from contextlib import ExitStack

import concourse.mybir as mybir

K, T, S, V, H, C = 512, 2048, 512, 256, 512, 512
FLOPS = 2 * K * H * S + 2 * K * C * V

F32 = mybir.dt.float32
BF16 = mybir.dt.bfloat16
I32 = mybir.dt.int32
U32 = mybir.dt.uint32
U16 = mybir.dt.uint16
U8 = mybir.dt.uint8
FP8X4 = mybir.dt.float8_e4m3fn_x4
ALU = mybir.AluOpType
ACT = mybir.ActivationFunctionType

P = 128
PACK = 4
HALF_M = 64
HALF_V = V // 2


def tile_picked_bondang_none_p_kernel(tc, x_words, x_scales, w1, gs, offs, i_l, k_l, j_l, cand, out):
    nc = tc.nc
    with ExitStack() as ctx:
        keep = ctx.enter_context(tc.tile_pool(name="keep", bufs=1))
        psum = ctx.enter_context(tc.psum_pool(name="psum", bufs=1))

        def load_list(name, src):
            tile = keep.tile(list(src.shape), U16, name=name)
            nc.sync.dma_start(tile[:], src)
            return tile

        table_scales = keep.tile([P, T], U8, name="table_scales", align_bytes=64)
        nc.vector.memset(table_scales[:].bitcast(I32), 0)
        quarter = keep.tile([P, 1], F32, name="quarter")
        nc.gpsimd.memset(quarter[:], 0.25)

        w_view = w1.rearrange("(p j) c -> p j c", j=PACK)
        w_raw = [keep.tile([P, PACK, H // 2], F32, name=f"w_raw{h}") for h in range(2)]
        offs_sb = load_list("offs_sb", offs)
        nc.sync.dma_start(w_raw[0][:], w_view[:, :, : H // 2])
        for q in range(4):
            nc.sync.dma_start(table_scales[32 * q : 32 * q + 4, :].bitcast(I32), x_scales[0, 4 * q : 4 * q + 4, :].bitcast(I32))
        cand_sb = load_list("cand_sb", cand)
        nc.sync.dma_start(w_raw[1][:], w_view[:, :, H // 2 :])
        table_words = keep.tile([P, T], I32, name="table_words", align_bytes=64)
        nc.sync.dma_start(table_words[:], x_words[0].rearrange("p n r -> p (n r)").bitcast(I32))
        k_sb = load_list("k_sb", k_l)
        i_sb = load_list("i_sb", i_l)
        j_sb = load_list("j_sb", j_l)
        gs_sb = keep.tile([P, PACK], F32, name="gs_sb")
        nc.sync.dma_start(gs_sb[:], gs.rearrange("(p t) o -> p (t o)", t=PACK))

        warm = keep.tile([P, 1], F32, name="warm")
        nc.scalar.activation(warm[:], quarter[:], ACT.Abs_reciprocal_sqrt, bias=quarter[:])

        def gather_packed(name, table, dtype, offsets):
            picked = keep.tile([P, S], dtype, name=name, align_bytes=64)
            nc.vector.tensor_copy(picked[:], table.indirect(offsets[:]))
            return picked

        xq_scales = gather_packed("xq_scales", table_scales[:], U8, offs_sb)
        xc_scales = gather_packed("xc_scales", table_scales[:], U8, cand_sb)

        w_codes = keep.tile([P, H], U32, name="w_codes", align_bytes=64)
        w_scales = keep.tile([P, H], U8, name="w_scales", align_bytes=64)
        grouped = keep.tile([P, PACK, P, PACK], BF16, name="w_grouped", align_bytes=64)
        for h in range(2):
            nc.scalar.copy(
                grouped[:, :, h * HALF_M : (h + 1) * HALF_M, :].rearrange("p t m j -> p m t j"),
                w_raw[h][:].rearrange("p j (m t) -> p m t j", t=PACK),
            )
        nc.vector.quantize_mx(
            out=w_codes[:].bitcast(FP8X4),
            scales=w_scales[:],
            in_=grouped[:].rearrange("p t m j -> p (t m j)"),
        )

        xq_words = keep.tile([P, S], U32, name="xq_words", align_bytes=64)
        for h in range(2):
            nc.vector.tensor_copy(
                xq_words[:, h * (S // 2) : (h + 1) * (S // 2)],
                table_words[:].bitcast(U32).indirect(offs_sb[:, h * (S // 32) : (h + 1) * (S // 32)]),
            )
        xc_words = gather_packed("xc_words", table_words[:].bitcast(U32), U32, cand_sb)

        def project(t, cols, name):
            acc = psum.tile([P, cols.stop - cols.start], F32, name=name)
            rows = slice(t * P, (t + 1) * P)
            nc.tensor.matmul_mx(
                out=acc[:],
                lhsT=w_codes[:, rows].bitcast(FP8X4),
                lhsT_scale=w_scales[:, rows],
                rhs=xq_words[:, cols].bitcast(FP8X4),
                rhs_scale=xq_scales[:, cols],
                start=True,
                stop=True,
            )
            return acc

        y = [keep.tile([P, S], F32, name=f"y{t}") for t in range(PACK)]
        lo, hi = slice(0, S // 2), slice(S // 2, S)
        nc.scalar.copy(y[0][:, lo], project(0, lo, "y0_lo")[:])
        nc.scalar.copy(y[0][:, hi], project(0, hi, "y0_hi")[:])
        for t in range(1, PACK):
            nc.scalar.copy(y[t][:], project(t, slice(0, S), f"y{t}_acc")[:])

        tip = [keep.tile([P, V], F32, name=f"tip{t}") for t in range(PACK)]
        prod = keep.tile([P, PACK, V], F32, name="prod")
        inv = keep.tile([P, PACK, V], F32, name="inv")

        def gather_tip(t, v0, n):
            nc.vector.tensor_copy(tip[t][:, v0 : v0 + n], y[t][:].indirect(k_sb[:, v0 // 16 : (v0 + n) // 16]))

        ab = [keep.tile([P, 2, V], F32, name=f"ab{t}") for t in range(PACK)]
        squares = [keep.tile([P, 2, V], F32, name=f"squares{t}") for t in range(PACK)]
        roots = keep.tile([P, PACK, 2, V], F32, name="roots")

        def bond(t, s, v0, n):
            lst = (i_sb, j_sb)[s]
            nc.vector.tensor_tensor(ab[t][:, s, v0 : v0 + n], y[t][:].indirect(lst[:, v0 // 16 : (v0 + n) // 16]), tip[t][:, v0 : v0 + n], ALU.subtract)

        def square(t, v0, n):
            nc.scalar.activation(squares[t][:, :, v0 : v0 + n], ab[t][:, :, v0 : v0 + n], ACT.Square)

        def root(t, v0, n):
            nc.scalar.activation(roots[:, t, :, v0 : v0 + n], squares[t][:, :, v0 : v0 + n], ACT.Abs_reciprocal_sqrt, bias=quarter[:])

        def numerator(t, v0, n):
            nc.vector.scalar_tensor_tensor(prod[:, t, v0 : v0 + n], ab[t][:, 0, v0 : v0 + n], gs_sb[:, t : t + 1], ab[t][:, 1, v0 : v0 + n], ALU.mult, ALU.mult)

        def denominator(t0, t1, v0, n):
            nc.vector.tensor_tensor(inv[:, t0:t1, v0 : v0 + n], roots[:, t0:t1, 0, v0 : v0 + n], roots[:, t0:t1, 1, v0 : v0 + n], ALU.mult)

        def weigh(h):
            vs = slice(h * HALF_V, (h + 1) * HALF_V)
            z = keep.tile([P, HALF_V, PACK], BF16, name=f"z{h}", align_bytes=64)
            nc.vector.tensor_tensor(
                z[:].rearrange("p (c i) t -> p c t i", i=4),
                prod[:, :, vs].rearrange("p t (c i) -> p c t i", i=4),
                inv[:, :, vs].rearrange("p t (c i) -> p c t i", i=4),
                ALU.mult,
            )
            return z

        def quantize_z(h, z):
            codes = keep.tile([P, HALF_V], U32, name=f"z_codes{h}", align_bytes=64)
            scales = keep.tile([P, HALF_V], U8, name=f"z_scales{h}", align_bytes=64)
            nc.vector.quantize_mx(out=codes[:].bitcast(FP8X4), scales=scales[:], in_=z[:].rearrange("p v t -> p (v t)"))
            return codes, scales

        out_view = out.rearrange("(b p) v -> p b v", p=P)

        def score(h, codes, scales, blocks, name):
            acc = psum.tile([P, len(blocks), HALF_V], F32, name=name)
            for n, b in enumerate(blocks):
                rows = slice(b * P, (b + 1) * P)
                nc.tensor.matmul_mx(
                    out=acc[:, n, :],
                    lhsT=xc_words[:, rows].bitcast(FP8X4),
                    lhsT_scale=xc_scales[:, rows],
                    rhs=codes[:].bitcast(FP8X4),
                    rhs_scale=scales[:],
                    start=True,
                    stop=True,
                )
            return acc

        def store(h, acc, blocks, on_vector):
            res = keep.tile([P, len(blocks), HALF_V], F32, name=f"res{h}_{blocks[0]}")
            if on_vector:
                nc.vector.tensor_scalar(res[:], acc[:], 0.0625, None, ALU.mult)
            else:
                nc.scalar.activation(res[:], acc[:], ACT.Copy, scale=0.0625)
            queue = nc.sync if on_vector or h == 0 else nc.scalar
            queue.dma_start(out_view[:, blocks[0] : blocks[-1] + 1, h * HALF_V : (h + 1) * HALF_V], res[:])

        gather_tip(0, 0, HALF_V)
        gather_tip(0, HALF_V, HALF_V)
        gather_tip(1, 0, V)
        bond(0, 0, 0, HALF_V)
        bond(0, 0, HALF_V, HALF_V)
        bond(0, 1, 0, V)
        square(0, 0, V)
        root(0, 0, V)
        gather_tip(2, 0, V)
        numerator(0, 0, V)
        bond(1, 0, 0, V)
        bond(1, 1, 0, V)
        square(1, 0, V)
        root(1, 0, V)
        gather_tip(3, 0, V)
        numerator(1, 0, V)
        bond(2, 0, 0, V)
        bond(2, 1, 0, V)
        square(2, 0, V)
        bond(3, 0, 0, HALF_V)
        bond(3, 1, 0, HALF_V)
        square(3, 0, HALF_V)
        root(3, 0, HALF_V)
        root(2, 0, V)
        bond(3, 0, HALF_V, HALF_V)
        bond(3, 1, HALF_V, HALF_V)
        square(3, HALF_V, HALF_V)
        root(3, HALF_V, HALF_V)
        numerator(3, 0, HALF_V)
        numerator(2, 0, V)
        numerator(3, HALF_V, HALF_V)
        denominator(3, 4, 0, HALF_V)
        denominator(0, 3, 0, HALF_V)
        denominator(0, 3, HALF_V, HALF_V)
        z0 = weigh(0)
        denominator(3, 4, HALF_V, HALF_V)
        q0 = quantize_z(0, z0)
        z1 = weigh(1)
        store(0, score(0, q0[0], q0[1], [0, 1, 2, 3], "out0"), [0, 1, 2, 3], False)
        q1 = quantize_z(1, z1)
        store(1, score(1, q1[0], q1[1], [0, 1], "out1a"), [0, 1], False)
        store(1, score(1, q1[0], q1[1], [2, 3], "out1b"), [2, 3], True)
